import numpy as np
import ml_dtypes


def mxq(x, axis, fmt="e4m3"):
    dtype, down = {"e4m3": (ml_dtypes.float8_e4m3fn, 7), "e5m2": (ml_dtypes.float8_e5m2, 14)}[fmt]
    v = np.moveaxis(np.asarray(x, np.float32).astype(ml_dtypes.bfloat16).astype(np.float64), axis, -1)
    blocks = v.reshape(v.shape[:-1] + (-1, 32))
    amax = np.abs(blocks).max(-1, keepdims=True)
    byte = np.maximum(np.where(amax > 0, np.frexp(amax)[1] - 1 + 127, 0) - down, 1)
    scale = np.exp2(byte - 127.0)
    codes = (blocks / scale).astype(np.float32).astype(dtype).astype(np.float64)
    return np.moveaxis((codes * scale).reshape(v.shape), -1, axis)


WIDE = False


def mx_kscale(k):
    if not WIDE:
        return np.ones(k)
    levels = np.array([10, -10, 5, -5, 0])
    if k % 512:
        return np.exp2(np.random.permutation(np.resize(levels, k // 32))).repeat(32)
    a = np.empty((k // 512, 16))
    for p in range(k // 512):
        a[p, :8] = np.random.permutation(np.resize(levels, 8))
        for g in range(8):
            far = levels[np.abs(levels - a[p, g]) >= 10]
            a[p, g + 8] = far[np.random.randint(len(far))]
    return np.exp2(a.ravel()).repeat(32)


def f64(x):
    return np.asarray(x).astype(np.float64)


def striped(idx):
    return np.tile(np.asarray(idx).reshape(-1, 16).T, (8, 1)).astype(np.uint16)


def unstriped(offs):
    return offs[:16].T.reshape(-1).astype(np.int64)


E2M1 = np.array([0.0, 0.5, 1.0, 1.5, 2.0, 3.0, 4.0, 6.0, -0.0, -0.5, -1.0, -1.5, -2.0, -3.0, -4.0, -6.0])


def pack_weight(w, fmt):
    k, n = w.shape
    w = f64(np.asarray(w, np.float32).astype(ml_dtypes.bfloat16)).reshape(k // 32, 32, n)
    amax = np.abs(w).max(1)
    if fmt == "e4m3":
        byte = np.frexp(amax)[1] - 1 + 127 - 7
    else:
        mant, ex = np.frexp(amax / 6.0)
        byte = np.where(mant > 0.5, ex, ex - 1) + 127
    byte = np.clip(np.where(amax > 0, byte, 1), 1, 254)
    scaled = (w * np.exp2(127.0 - byte)[:, None, :]).reshape(k, n).astype(np.float32)
    by_word = np.ascontiguousarray(scaled.reshape(k // 512, 128, 4, n).transpose(0, 1, 3, 2))
    if fmt == "e4m3":
        words = by_word.astype(ml_dtypes.float8_e4m3fn).view(np.uint8)
    else:
        c = by_word.astype(ml_dtypes.float4_e2m1fn).view(np.uint8) & 0xF
        words = (c[..., 0::2] | (c[..., 1::2] << 4)).reshape(k // 512, 128, 2 * n)
    return np.ascontiguousarray(words), np.ascontiguousarray(byte.astype(np.uint8).reshape(k // 512, 16, n))


def unpack_weight(words, scales, fmt):
    g, _, n = scales.shape
    words = np.ascontiguousarray(words).reshape(g, 128, n, -1)
    if fmt == "e4m3":
        vals = words.view(ml_dtypes.float8_e4m3fn).astype(np.float64)
    else:
        nib = np.empty((g, 128, n, 4), np.uint8)
        nib[..., 0::2] = words & 0xF
        nib[..., 1::2] = words >> 4
        vals = E2M1[nib]
    vals = vals * np.repeat(np.exp2(scales.astype(np.float64) - 127.0), 8, axis=1)[..., None]
    return vals.transpose(0, 1, 3, 2).reshape(g * 512, n)


D, T, I, Q, E, M = 512, 2048, 512, 512, 512, 1024


def setup_inputs():
    n = np.random.standard_normal
    idx = np.random.permutation(T)[:I]
    idx2 = np.random.randint(0, Q, M)
    fd = mx_kscale(D)
    fi = mx_kscale(I)
    ti = np.ones(T)
    ti[idx] = fi
    keysp = pack_weight(n((D, T)) / fd[:, None], "e4m3")
    return {
        "query": (n((D, Q)) * 0.4 / np.sqrt(D) * fd[:, None]).astype(np.float32),
        "keys_words": keysp[0],
        "keys_scales": keysp[1],
        "size": (np.random.uniform(0.5, 2.0, (1, I)) * fi).astype(np.float32),
        "vals": (n((E, T)) / ti).astype(np.float32),
        "offs": striped(idx),
        "offs2": striped(idx2),
    }


def reference(query, keys_words, keys_scales, size, vals, offs, offs2):
    idx = unstriped(offs)
    idx2 = unstriped(offs2)
    keysu = unpack_weight(keys_words, keys_scales, "e4m3")
    queryq = mxq(f64(query), 0, "e4m3")
    keysidxg = keysu[:, idx]
    a = queryq.T @ keysidxg
    p = np.exp(a - np.max(a, axis=1, keepdims=True))
    w = p * f64(size) / np.sum(p, axis=1, keepdims=True)
    wt = w.T
    vt = f64(vals)[:, idx].T
    vtq = mxq(vt, 0, "e4m3")
    wtq = mxq(wt, 0, "e4m3")
    o = vtq.T @ wtq
    y = o[:, idx2]
    return y

@@ -1,0 +1,170 @@
+from contextlib import ExitStack
+
+import concourse.mybir as mybir
+from concourse.masks import make_identity
+
+F32 = mybir.dt.float32
+BF16 = mybir.dt.bfloat16
+I32 = mybir.dt.int32
+U32 = mybir.dt.uint32
+U16 = mybir.dt.uint16
+U8 = mybir.dt.uint8
+FP8X4 = mybir.dt.float8_e4m3fn_x4
+ACT = mybir.ActivationFunctionType
+ALU = mybir.AluOpType
+AXIS = mybir.AxisListType
+
+P = 128
+D, T, I, Q, E, M = 512, 2048, 512, 512, 512, 1024
+FLOPS = 2 * D * Q * I + 2 * I * E * Q
+NB = 4
+PIECE = 256
+
+
+def tile_attend_unmerge_kernel(tc, query, keys_words, keys_scales, size, vals, offs, offs2, out):
+    nc = tc.nc
+    with ExitStack() as ctx:
+        held = ctx.enter_context(tc.tile_pool(name="held", bufs=1))
+        ring = ctx.enter_context(tc.tile_pool(name="ring", bufs=4))
+        psum = ctx.enter_context(tc.psum_pool(name="psum", bufs=1))
+        acc_pool = ctx.enter_context(tc.psum_pool(name="acc", bufs=4))
+        turn_pool = ctx.enter_context(tc.psum_pool(name="turn", bufs=3))
+
+        slots = held.tile([P, I // 16], U16, name="slots")
+        rows = held.tile([P, M // 16], U16, name="rows")
+        key_words = ring.tile([P, T], U32, name="key_words", tag="inputs")
+        key_bytes = ring.tile([P, T], U8, name="key_bytes", tag="inputs")
+        q_raw = [ring.tile([P, 4, Q // 2], F32, name=f"q_raw{h}", tag="inputs") for h in range(2)]
+        size_cols = held.tile([P, 4], F32, name="size_cols")
+        v_raw = [ring.tile([P, T], F32, name=f"v_raw{j}", tag="inputs") for j in range(NB)]
+        ident = held.tile([P, P], F32, name="ident")
+
+        warm = held.tile([P, 2], F32, name="warm")
+        nc.gpsimd.memset(key_bytes[:].bitcast(I32), 0)
+        nc.gpsimd.memset(warm[:], 0.0)
+        nc.sync.dma_start(slots[:], offs)
+        nc.sync.dma_start(key_words[:].bitcast(I32), keys_words[0].rearrange("p n t -> p (n t)").bitcast(I32))
+        for g in range(4):
+            nc.scalar.dma_start(key_bytes[32 * g : 32 * g + 4, :].bitcast(I32), keys_scales[0, 4 * g : 4 * g + 4, :].bitcast(I32))
+        nc.sync.dma_start(rows[:], offs2)
+        q_view = query.rearrange("(p j) q -> p j q", j=4)
+        for h in range(2):
+            nc.sync.dma_start(q_raw[h][:], q_view[:, :, h * (Q // 2) : (h + 1) * (Q // 2)])
+        for j in range(NB):
+            nc.sync.dma_start(v_raw[j][:], vals[j * P : (j + 1) * P, :])
+        nc.scalar.activation(warm[:, 1:2], warm[:, 0:1], ACT.Exp)
+        nc.gpsimd.dma_start(size_cols[:], size.rearrange("o (s t) -> (o s) t", t=4))
+        make_identity(nc, ident[:])
+
+        o_tiles = [held.tile([P, Q + 16], F32, name=f"o{j}") for j in range(NB)]
+        for j in range(NB):
+            nc.gpsimd.memset(o_tiles[j][:, Q : Q + 16], 0.0)
+        k_codes = held.tile([P, I], U32, name="k_codes", align_bytes=64)
+        k_scales = held.tile([P, I], U8, name="k_scales", align_bytes=64)
+        nc.vector.tensor_copy(k_scales[:], key_bytes[:].indirect(slots[:]))
+        nc.vector.tensor_copy(k_codes[:], key_words[:].indirect(slots[:]))
+
+        size_wide = psum.tile([P, 4, P], F32, name="size_wide")
+        for t in range(4):
+            nc.tensor.transpose(size_wide[:, t, :], size_cols[:, t : t + 1].to_broadcast([P, P]), ident[:])
+
+        w_codes = held.tile([P, Q], U32, name="w_codes", align_bytes=64)
+        w_scales = held.tile([P, Q], U8, name="w_scales", align_bytes=64)
+
+        def turn(src, name):
+            words = src[:].bitcast(F32)
+            turned = turn_pool.tile([P, 2, P], F32, name="turned")
+            for u in range(2):
+                nc.tensor.transpose(turned[:, u, :], words[:, u : 2 * P : 2], ident[:])
+            grouped = held.tile([P, 4 * P], BF16, name=name, tag=name, align_bytes=64)
+            nc.scalar.copy(grouped[:].bitcast(F32).rearrange("p (c u) -> p c u", u=2), turned[:].rearrange("p u c -> p c u"))
+            return grouped
+
+        def group_query(b):
+            grouped = held.tile([P, P, 4], BF16, name=f"q_grouped{b}", align_bytes=64)
+            src = q_raw[b // 2][:, :, (b % 2) * P : (b % 2 + 1) * P].rearrange("p j (c i) -> p c j i", i=4)
+            dst = grouped[:].rearrange("p (c i) j -> p c j i", i=4)
+            if b == 0:
+                nc.vector.tensor_copy(dst, src)
+            else:
+                nc.scalar.copy(dst, src)
+            return grouped
+
+        def score(b, grouped):
+            codes = held.tile([P, P], U32, name=f"q_codes{b}", align_bytes=64)
+            scales = held.tile([P, P], U8, name=f"q_scales{b}", align_bytes=64)
+            nc.vector.quantize_mx(out=codes[:].bitcast(FP8X4), scales=scales[:], in_=grouped[:].rearrange("p c j -> p (c j)"))
+            a = acc_pool.tile([P, I], F32, name="acc")
+            nc.tensor.matmul_mx(out=a[:], lhsT=codes[:].bitcast(FP8X4), lhsT_scale=scales[:], rhs=k_codes[:].bitcast(FP8X4), rhs_scale=k_scales[:], start=True, stop=True)
+            return a
+
+        def exponentials(b, a):
+            neg_max = held.tile([P, 1], F32, name=f"neg_max{b}")
+            nc.vector.tensor_reduce(neg_max[:], a[:], AXIS.X, ALU.max, negate=True)
+            p = held.tile([P, I], F32, name=f"p{b}", tag=f"p{b}", align_bytes=64)
+            total = held.tile([P, 1], F32, name=f"total{b}")
+            nc.scalar.activation(p[:], a[:], ACT.Exp, bias=neg_max[:], accum_out=total[:])
+            return p, total
+
+        def weigh(b, p, total):
+            inverse = held.tile([P, 1], F32, name=f"inverse{b}")
+            nc.vector.reciprocal(inverse[:], total[:])
+            w = held.tile([P, I], BF16, name=f"w{b}")
+            nc.vector.scalar_tensor_tensor(
+                w[:].rearrange("p (s t) -> p s t", t=4), p[:].rearrange("p (s t) -> p s t", t=4), inverse[:],
+                size_wide[:].rearrange("p t s -> p s t"), ALU.mult, ALU.mult,
+            )
+            return turn(w, f"w_grouped{b}")
+
+        def quantise_w(b, grouped):
+            cols = slice(b * P, (b + 1) * P)
+            nc.vector.quantize_mx(out=w_codes[:, cols].bitcast(FP8X4), scales=w_scales[:, cols], in_=grouped[:])
+
+        def gather_v(j):
+            picked = held.tile([P, I], BF16, name=f"v_picked{j}", tag=["p3", "w_grouped3", "v_grouped0", "v_grouped1"][j], align_bytes=64)
+            nc.vector.tensor_copy(picked[:], v_raw[j][:].indirect(slots[:]))
+            return turn(picked, f"v_grouped{j}")
+
+        def multiply(j, grouped):
+            codes = held.tile([P, P], U32, name=f"v_codes{j}", align_bytes=64)
+            scales = held.tile([P, P], U8, name=f"v_scales{j}", align_bytes=64)
+            nc.vector.quantize_mx(out=codes[:].bitcast(FP8X4), scales=scales[:], in_=grouped[:])
+            acc = acc_pool.tile([P, Q], F32, name="acc")
+            nc.tensor.matmul_mx(out=acc[:], lhsT=codes[:].bitcast(FP8X4), lhsT_scale=scales[:], rhs=w_codes[:].bitcast(FP8X4), rhs_scale=w_scales[:], start=True, stop=True)
+            nc.scalar.copy(o_tiles[j][:, 0:Q], acc[:])
+            return o_tiles[j]
+
+        def unmerge(j, o, widths):
+            first = 0
+            for h, width in enumerate(widths):
+                y = held.tile([P, width], F32, name=f"y{j}_{h}")
+                nc.vector.tensor_copy(y[:], o[:].indirect(rows[:, first // 16 : (first + width) // 16]))
+                nc.sync.dma_start(out[j * P : (j + 1) * P, first : first + width], y[:])
+                first = first + width
+
+        qg = [group_query(b) for b in range(2)]
+        scores = [score(b, qg[b]) for b in range(2)]
+        qg.append(group_query(2))
+        ps = [exponentials(0, scores[0])]
+        scores.append(score(2, qg[2]))
+        qg.append(group_query(3))
+        ps.append(exponentials(1, scores[1]))
+        scores.append(score(3, qg[3]))
+        ps.append(exponentials(2, scores[2]))
+        wg = [weigh(0, ps[0][0], ps[0][1])]
+        ps.append(exponentials(3, scores[3]))
+        wg = wg + [weigh(b, ps[b][0], ps[b][1]) for b in range(1, NB)]
+        vg = [gather_v(0)]
+        for b in range(NB):
+            quantise_w(b, wg[b])
+        vg.append(gather_v(1))
+        outs = [multiply(0, vg[0])]
+        vg.append(gather_v(2))
+        outs.append(multiply(1, vg[1]))
+        unmerge(0, outs[0], [512, 512])
+        vg.append(gather_v(3))
+        outs.append(multiply(2, vg[2]))
+        unmerge(1, outs[1], [512, 512])
+        outs.append(multiply(3, vg[3]))
+        unmerge(2, outs[2], [512, 512])
+        unmerge(3, outs[3], [512, 256, 256])

@@ -18,153 +18,176 @@ P = 128
 D, T, I, Q, E, M = 512, 2048, 512, 512, 512, 1024
 FLOPS = 2 * D * Q * I + 2 * I * E * Q
 NB = 4
-PIECE = 256
+SPARE = 16
 
 
 def tile_attend_unmerge_kernel(tc, query, keys_words, keys_scales, size, vals, offs, offs2, out):
     nc = tc.nc
     with ExitStack() as ctx:
         held = ctx.enter_context(tc.tile_pool(name="held", bufs=1))
-        ring = ctx.enter_context(tc.tile_pool(name="ring", bufs=4))
         psum = ctx.enter_context(tc.psum_pool(name="psum", bufs=1))
         acc_pool = ctx.enter_context(tc.psum_pool(name="acc", bufs=4))
         turn_pool = ctx.enter_context(tc.psum_pool(name="turn", bufs=3))
 
+        def sbuf(shape, dtype, name, after=None):
+            return held.tile(shape, dtype, name=name, tag=after or name, align_bytes=64)
+
         slots = held.tile([P, I // 16], U16, name="slots")
         rows = held.tile([P, M // 16], U16, name="rows")
-        key_words = ring.tile([P, T], U32, name="key_words", tag="inputs")
-        key_bytes = ring.tile([P, T], U8, name="key_bytes", tag="inputs")
-        q_raw = [ring.tile([P, 4, Q // 2], F32, name=f"q_raw{h}", tag="inputs") for h in range(2)]
-        size_cols = held.tile([P, 4], F32, name="size_cols")
-        v_raw = [ring.tile([P, T], F32, name=f"v_raw{j}", tag="inputs") for j in range(NB)]
-        ident = held.tile([P, P], F32, name="ident")
-
-        warm = held.tile([P, 2], F32, name="warm")
+        key_words = sbuf([P, T], U32, "key_words")
+        key_bytes = sbuf([P, T], U8, "key_bytes")
+        ident = sbuf([P, P], F32, "ident")
         nc.gpsimd.memset(key_bytes[:].bitcast(I32), 0)
-        nc.gpsimd.memset(warm[:], 0.0)
+        make_identity(nc, ident[:])
         nc.sync.dma_start(slots[:], offs)
         nc.sync.dma_start(key_words[:].bitcast(I32), keys_words[0].rearrange("p n t -> p (n t)").bitcast(I32))
         for g in range(4):
             nc.scalar.dma_start(key_bytes[32 * g : 32 * g + 4, :].bitcast(I32), keys_scales[0, 4 * g : 4 * g + 4, :].bitcast(I32))
-        nc.sync.dma_start(rows[:], offs2)
         q_view = query.rearrange("(p j) q -> p j q", j=4)
+        q_raw = [sbuf([P, 4, Q // 2], F32, f"q_raw{h}") for h in range(2)]
         for h in range(2):
             nc.sync.dma_start(q_raw[h][:], q_view[:, :, h * (Q // 2) : (h + 1) * (Q // 2)])
-        for j in range(NB):
-            nc.sync.dma_start(v_raw[j][:], vals[j * P : (j + 1) * P, :])
-        nc.scalar.activation(warm[:, 1:2], warm[:, 0:1], ACT.Exp)
-        nc.gpsimd.dma_start(size_cols[:], size.rearrange("o (s t) -> (o s) t", t=4))
-        make_identity(nc, ident[:])
+        nc.sync.dma_start(rows[:], offs2)
 
-        o_tiles = [held.tile([P, Q + 16], F32, name=f"o{j}") for j in range(NB)]
+        def load_v(j, after):
+            raw = sbuf([P, T], F32, f"v_raw{j}", after=after)
+            nc.sync.dma_start(raw[:], vals[j * P : (j + 1) * P, :])
+            return raw
+
+        o_tiles = [sbuf([P, Q + SPARE], F32, f"o{j}") for j in range(NB)]
         for j in range(NB):
-            nc.gpsimd.memset(o_tiles[j][:, Q : Q + 16], 0.0)
-        k_codes = held.tile([P, I], U32, name="k_codes", align_bytes=64)
-        k_scales = held.tile([P, I], U8, name="k_scales", align_bytes=64)
-        nc.vector.tensor_copy(k_scales[:], key_bytes[:].indirect(slots[:]))
+            nc.gpsimd.memset(o_tiles[j][:, Q : Q + SPARE], 0.0)
+
+        k_codes = sbuf([P, I], U32, "k_codes")
+        k_scales = sbuf([P, I], U8, "k_scales")
         nc.vector.tensor_copy(k_codes[:], key_words[:].indirect(slots[:]))
+        nc.vector.tensor_copy(k_scales[:], key_bytes[:].indirect(slots[:]))
 
+        v_raw = {3: load_v(3, "key_words")}
+        size_cols = sbuf([P, 4], F32, "size_cols", after="key_bytes")
+        nc.sync.dma_start(size_cols[:], size.rearrange("o (s t) -> (o s) t", t=4))
         size_wide = psum.tile([P, 4, P], F32, name="size_wide")
         for t in range(4):
             nc.tensor.transpose(size_wide[:, t, :], size_cols[:, t : t + 1].to_broadcast([P, P]), ident[:])
 
-        w_codes = held.tile([P, Q], U32, name="w_codes", align_bytes=64)
-        w_scales = held.tile([P, Q], U8, name="w_scales", align_bytes=64)
-
-        def turn(src, name):
+        def turn(src, dst):
             words = src[:].bitcast(F32)
             turned = turn_pool.tile([P, 2, P], F32, name="turned")
             for u in range(2):
                 nc.tensor.transpose(turned[:, u, :], words[:, u : 2 * P : 2], ident[:])
-            grouped = held.tile([P, 4 * P], BF16, name=name, tag=name, align_bytes=64)
-            nc.scalar.copy(grouped[:].bitcast(F32).rearrange("p (c u) -> p c u", u=2), turned[:].rearrange("p u c -> p c u"))
-            return grouped
+            nc.scalar.copy(dst.bitcast(F32).rearrange("p (c u) -> p c u", u=2), turned[:].rearrange("p u c -> p c u"))
 
-        def group_query(b):
-            grouped = held.tile([P, P, 4], BF16, name=f"q_grouped{b}", align_bytes=64)
+        def quantise(grouped, name, after=None):
+            columns = grouped.shape[1] // 4
+            codes = sbuf([P, columns], U32, name + "_codes", after=after)
+            scales = sbuf([P, columns], U8, name + "_scales")
+            nc.vector.quantize_mx(out=codes[:].bitcast(FP8X4), scales=scales[:], in_=grouped[:])
+            return codes, scales
+
+        def product(lhs, cols, rhs):
+            acc = acc_pool.tile([P, 512], F32, name="acc")
+            nc.tensor.matmul_mx(out=acc[:], lhsT=lhs[0][:, cols].bitcast(FP8X4), lhsT_scale=lhs[1][:, cols], rhs=rhs[0][:].bitcast(FP8X4), rhs_scale=rhs[1][:], start=True, stop=True)
+            return acc
+
+        def group_queries(b):
+            grouped = sbuf([P, 4 * P], BF16, f"q_grouped{b}")
             src = q_raw[b // 2][:, :, (b % 2) * P : (b % 2 + 1) * P].rearrange("p j (c i) -> p c j i", i=4)
-            dst = grouped[:].rearrange("p (c i) j -> p c j i", i=4)
-            if b == 0:
-                nc.vector.tensor_copy(dst, src)
-            else:
-                nc.scalar.copy(dst, src)
+            nc.scalar.activation(grouped[:].rearrange("p (c i j) -> p c j i", i=4, j=4), src, ACT.Copy)
             return grouped
 
         def score(b, grouped):
-            codes = held.tile([P, P], U32, name=f"q_codes{b}", align_bytes=64)
-            scales = held.tile([P, P], U8, name=f"q_scales{b}", align_bytes=64)
-            nc.vector.quantize_mx(out=codes[:].bitcast(FP8X4), scales=scales[:], in_=grouped[:].rearrange("p c j -> p (c j)"))
-            a = acc_pool.tile([P, I], F32, name="acc")
-            nc.tensor.matmul_mx(out=a[:], lhsT=codes[:].bitcast(FP8X4), lhsT_scale=scales[:], rhs=k_codes[:].bitcast(FP8X4), rhs_scale=k_scales[:], start=True, stop=True)
-            return a
+            return product(quantise(grouped, f"q{b}"), slice(0, P), (k_codes, k_scales))
 
         def exponentials(b, a):
-            neg_max = held.tile([P, 1], F32, name=f"neg_max{b}")
+            neg_max = sbuf([P, 1], F32, f"neg_max{b}")
             nc.vector.tensor_reduce(neg_max[:], a[:], AXIS.X, ALU.max, negate=True)
-            p = held.tile([P, I], F32, name=f"p{b}", tag=f"p{b}", align_bytes=64)
-            total = held.tile([P, 1], F32, name=f"total{b}")
+            p = sbuf([P, I], F32, f"p{b}")
+            total = sbuf([P, 1], F32, f"total{b}")
             nc.scalar.activation(p[:], a[:], ACT.Exp, bias=neg_max[:], accum_out=total[:])
             return p, total
 
-        def weigh(b, p, total):
-            inverse = held.tile([P, 1], F32, name=f"inverse{b}")
+        def invert(b, total):
+            inverse = sbuf([P, 1], F32, f"inverse{b}")
             nc.vector.reciprocal(inverse[:], total[:])
-            w = held.tile([P, I], BF16, name=f"w{b}")
+            return inverse
+
+        w_grouped = sbuf([P, 4 * Q], BF16, "w_grouped")
+
+        def weigh(b, p, inverse):
+            w = sbuf([P, I], BF16, f"w{b}")
             nc.vector.scalar_tensor_tensor(
                 w[:].rearrange("p (s t) -> p s t", t=4), p[:].rearrange("p (s t) -> p s t", t=4), inverse[:],
                 size_wide[:].rearrange("p t s -> p s t"), ALU.mult, ALU.mult,
             )
-            return turn(w, f"w_grouped{b}")
+            turn(w, w_grouped[:, b * 4 * P : (b + 1) * 4 * P])
 
-        def quantise_w(b, grouped):
-            cols = slice(b * P, (b + 1) * P)
-            nc.vector.quantize_mx(out=w_codes[:, cols].bitcast(FP8X4), scales=w_scales[:, cols], in_=grouped[:])
-
-        def gather_v(j):
-            picked = held.tile([P, I], BF16, name=f"v_picked{j}", tag=["p3", "w_grouped3", "v_grouped0", "v_grouped1"][j], align_bytes=64)
+        def pick_on_vector(j, after):
+            picked = sbuf([P, I], BF16, f"v_picked{j}", after=after)
             nc.vector.tensor_copy(picked[:], v_raw[j][:].indirect(slots[:]))
-            return turn(picked, f"v_grouped{j}")
+            return picked
 
-        def multiply(j, grouped):
-            codes = held.tile([P, P], U32, name=f"v_codes{j}", align_bytes=64)
-            scales = held.tile([P, P], U8, name=f"v_scales{j}", align_bytes=64)
-            nc.vector.quantize_mx(out=codes[:].bitcast(FP8X4), scales=scales[:], in_=grouped[:])
-            acc = acc_pool.tile([P, Q], F32, name="acc")
-            nc.tensor.matmul_mx(out=acc[:], lhsT=codes[:].bitcast(FP8X4), lhsT_scale=scales[:], rhs=w_codes[:].bitcast(FP8X4), rhs_scale=w_scales[:], start=True, stop=True)
+        def cast_on_scalar(j, after):
+            rounded = sbuf([P, T], BF16, f"v_rounded{j}", after=after)
+            for c in range(0, T, 512):
+                nc.scalar.activation(rounded[:, c : c + 512], v_raw[j][:, c : c + 512], ACT.Copy)
+            return rounded
+
+        def pick_on_scalar(picked, rounded, c):
+            nc.scalar.activation(picked[:, c : c + 256], rounded[:].indirect(slots[:, c // 16 : (c + 256) // 16]), ACT.Copy)
+
+        def turn_v(j, picked, after=None):
+            grouped = sbuf([P, 4 * P], BF16, f"v_grouped{j}", after=after)
+            turn(picked, grouped[:])
+            return grouped
+
+        def multiply(j, grouped, w_quantised, after=None):
+            acc = product(quantise(grouped, f"v{j}", after), slice(0, P), w_quantised)
             nc.scalar.copy(o_tiles[j][:, 0:Q], acc[:])
-            return o_tiles[j]
 
-        def unmerge(j, o, widths):
-            first = 0
-            for h, width in enumerate(widths):
-                y = held.tile([P, width], F32, name=f"y{j}_{h}")
-                nc.vector.tensor_copy(y[:], o[:].indirect(rows[:, first // 16 : (first + width) // 16]))
-                nc.sync.dma_start(out[j * P : (j + 1) * P, first : first + width], y[:])
-                first = first + width
+        def unmerge(j, first, width, after=None):
+            y = sbuf([P, width], F32, f"y{j}_{first}", after=after)
+            nc.vector.tensor_copy(y[:], o_tiles[j][:].indirect(rows[:, first // 16 : (first + width) // 16]))
+            nc.sync.dma_start(out[j * P : (j + 1) * P, first : first + width], y[:])
 
-        qg = [group_query(b) for b in range(2)]
-        scores = [score(b, qg[b]) for b in range(2)]
-        qg.append(group_query(2))
-        ps = [exponentials(0, scores[0])]
-        scores.append(score(2, qg[2]))
-        qg.append(group_query(3))
-        ps.append(exponentials(1, scores[1]))
-        scores.append(score(3, qg[3]))
-        ps.append(exponentials(2, scores[2]))
-        wg = [weigh(0, ps[0][0], ps[0][1])]
-        ps.append(exponentials(3, scores[3]))
-        wg = wg + [weigh(b, ps[b][0], ps[b][1]) for b in range(1, NB)]
-        vg = [gather_v(0)]
-        for b in range(NB):
-            quantise_w(b, wg[b])
-        vg.append(gather_v(1))
-        outs = [multiply(0, vg[0])]
-        vg.append(gather_v(2))
-        outs.append(multiply(1, vg[1]))
-        unmerge(0, outs[0], [512, 512])
-        vg.append(gather_v(3))
-        outs.append(multiply(2, vg[2]))
-        unmerge(1, outs[1], [512, 512])
-        outs.append(multiply(3, vg[3]))
-        unmerge(2, outs[2], [512, 512])
-        unmerge(3, outs[3], [512, 256, 256])
+        grouped = [group_queries(b) for b in range(3)]
+        a = [score(b, grouped[b]) for b in range(2)]
+        v_raw[0] = load_v(0, "q_grouped0")
+        v_raw[1] = load_v(1, "q_grouped1")
+        e0 = exponentials(0, a[0])
+        grouped.append(group_queries(3))
+        a.append(score(2, grouped[2]))
+        v_raw[2] = load_v(2, "q_grouped2")
+        e1 = exponentials(1, a[1])
+        a.append(score(3, grouped[3]))
+        r0 = invert(0, e0[1])
+        e2 = exponentials(2, a[2])
+        weigh(0, e0[0], r0)
+        r1 = invert(1, e1[1])
+        e3 = exponentials(3, a[3])
+        r2 = invert(2, e2[1])
+        weigh(1, e1[0], r1)
+        r3 = invert(3, e3[1])
+        weigh(2, e2[0], r2)
+        weigh(3, e3[0], r3)
+        rounded3 = cast_on_scalar(3, "neg_max3")
+        g0 = turn_v(0, pick_on_vector(0, "p3"))
+        w_quantised = quantise(w_grouped, "w")
+        multiply(0, g0, w_quantised)
+        g1 = turn_v(1, pick_on_vector(1, "v_grouped0"), "v0_codes")
+        picked3 = sbuf([P, I], BF16, "v_picked3", after="v0_scales")
+        pick_on_scalar(picked3, rounded3, 0)
+        pick_on_scalar(picked3, rounded3, 256)
+        unmerge(0, 0, 512)
+        multiply(1, g1, w_quantised)
+        unmerge(0, 512, 512, "v0_codes")
+        g3 = turn_v(3, picked3)
+        g2 = turn_v(2, pick_on_vector(2, "o0"), "v1_codes")
+        unmerge(1, 0, 512)
+        multiply(2, g2, w_quantised)
+        multiply(3, g3, w_quantised, "q_grouped2")
+        unmerge(1, 512, 512, "v1_codes")
+        unmerge(2, 0, 512)
+        unmerge(2, 512, 512)
+        unmerge(3, 0, 512)
+        unmerge(3, 512, 256)
+        unmerge(3, 768, 256)

@@ -66,9 +66,9 @@ def tile_attend_unmerge_kernel(tc, query, keys_words, keys_scales, size, vals, o
         v_raw = {3: load_v(3, "key_words")}
         size_cols = sbuf([P, 4], F32, "size_cols", after="key_bytes")
         nc.sync.dma_start(size_cols[:], size.rearrange("o (s t) -> (o s) t", t=4))
-        size_wide = psum.tile([P, 4, P], F32, name="size_wide")
+        size_wide = psum.tile([P, I], F32, name="size_wide")
         for t in range(4):
-            nc.tensor.transpose(size_wide[:, t, :], size_cols[:, t : t + 1].to_broadcast([P, P]), ident[:])
+            nc.tensor.transpose(size_wide[:, t:I:4], size_cols[:, t : t + 1].to_broadcast([P, P]), ident[:])
 
         def turn(src, dst):
             words = src[:].bitcast(F32)
@@ -115,10 +115,7 @@ def tile_attend_unmerge_kernel(tc, query, keys_words, keys_scales, size, vals, o
 
         def weigh(b, p, inverse):
             w = sbuf([P, I], BF16, f"w{b}")
-            nc.vector.scalar_tensor_tensor(
-                w[:].rearrange("p (s t) -> p s t", t=4), p[:].rearrange("p (s t) -> p s t", t=4), inverse[:],
-                size_wide[:].rearrange("p t s -> p s t"), ALU.mult, ALU.mult,
-            )
+            nc.vector.scalar_tensor_tensor(w[:], p[:], inverse[:], size_wide[:], ALU.mult, ALU.mult)
             turn(w, w_grouped[:, b * 4 * P : (b + 1) * 4 * P])
 
         def pick_on_vector(j, after):

@@ -37,17 +37,22 @@ def tile_attend_unmerge_kernel(tc, query, keys_words, keys_scales, size, vals, o
         key_words = sbuf([P, T], U32, "key_words")
         key_bytes = sbuf([P, T], U8, "key_bytes")
         ident = sbuf([P, P], F32, "ident")
+        scale_rows = sbuf([P, T], U8, "scale_rows")
         nc.gpsimd.memset(key_bytes[:].bitcast(I32), 0)
         make_identity(nc, ident[:])
         nc.sync.dma_start(slots[:], offs)
+        for g, queue in enumerate([nc.scalar, nc.sync, nc.scalar, nc.sync]):
+            queue.dma_start(scale_rows[32 * g : 32 * g + 4, :].bitcast(I32), keys_scales[0, 4 * g : 4 * g + 4, :].bitcast(I32))
+        size_cols = sbuf([P, 4], F32, "size_cols")
+        nc.scalar.dma_start(size_cols[:], size.rearrange("o (s t) -> (o s) t", t=4))
         nc.sync.dma_start(key_words[:].bitcast(I32), keys_words[0].rearrange("p n t -> p (n t)").bitcast(I32))
-        for g in range(4):
-            nc.scalar.dma_start(key_bytes[32 * g : 32 * g + 4, :].bitcast(I32), keys_scales[0, 4 * g : 4 * g + 4, :].bitcast(I32))
         q_view = query.rearrange("(p j) q -> p j q", j=4)
         q_raw = [sbuf([P, 4, Q // 2], F32, f"q_raw{h}") for h in range(2)]
         for h in range(2):
             nc.sync.dma_start(q_raw[h][:], q_view[:, :, h * (Q // 2) : (h + 1) * (Q // 2)])
         nc.sync.dma_start(rows[:], offs2)
+        for g in range(4):
+            nc.vector.tensor_copy(key_bytes[32 * g : 32 * g + 4, :].bitcast(I32), scale_rows[32 * g : 32 * g + 4, :].bitcast(I32))
 
         def load_v(j, after):
             raw = sbuf([P, T], F32, f"v_raw{j}", after=after)
@@ -58,14 +63,12 @@ def tile_attend_unmerge_kernel(tc, query, keys_words, keys_scales, size, vals, o
         for j in range(NB):
             nc.gpsimd.memset(o_tiles[j][:, Q : Q + SPARE], 0.0)
 
-        k_codes = sbuf([P, I], U32, "k_codes")
         k_scales = sbuf([P, I], U8, "k_scales")
-        nc.vector.tensor_copy(k_codes[:], key_words[:].indirect(slots[:]))
         nc.vector.tensor_copy(k_scales[:], key_bytes[:].indirect(slots[:]))
+        k_codes = sbuf([P, I], U32, "k_codes", after="key_bytes")
+        nc.vector.tensor_copy(k_codes[:], key_words[:].indirect(slots[:]))
 
         v_raw = {3: load_v(3, "key_words")}
-        size_cols = sbuf([P, 4], F32, "size_cols", after="key_bytes")
-        nc.sync.dma_start(size_cols[:], size.rearrange("o (s t) -> (o s) t", t=4))
         size_wide = psum.tile([P, I], F32, name="size_wide")
         for t in range(4):
             nc.tensor.transpose(size_wide[:, t:I:4], size_cols[:, t : t + 1].to_broadcast([P, P]), ident[:])
@@ -92,7 +95,11 @@ def tile_attend_unmerge_kernel(tc, query, keys_words, keys_scales, size, vals, o
         def group_queries(b):
             grouped = sbuf([P, 4 * P], BF16, f"q_grouped{b}")
             src = q_raw[b // 2][:, :, (b % 2) * P : (b % 2 + 1) * P].rearrange("p j (c i) -> p c j i", i=4)
-            nc.scalar.activation(grouped[:].rearrange("p (c i j) -> p c j i", i=4, j=4), src, ACT.Copy)
+            dst = grouped[:].rearrange("p (c i j) -> p c j i", i=4, j=4)
+            if b % 2 == 0:
+                nc.vector.tensor_copy(dst, src)
+            else:
+                nc.scalar.activation(dst, src, ACT.Copy)
             return grouped
 
         def score(b, grouped):
@@ -146,16 +153,15 @@ def tile_attend_unmerge_kernel(tc, query, keys_words, keys_scales, size, vals, o
             nc.vector.tensor_copy(y[:], o_tiles[j][:].indirect(rows[:, first // 16 : (first + width) // 16]))
             nc.sync.dma_start(out[j * P : (j + 1) * P, first : first + width], y[:])
 
-        grouped = [group_queries(b) for b in range(3)]
+        grouped = [group_queries(b) for b in range(2)]
         a = [score(b, grouped[b]) for b in range(2)]
-        v_raw[0] = load_v(0, "q_grouped0")
-        v_raw[1] = load_v(1, "q_grouped1")
-        e0 = exponentials(0, a[0])
-        grouped.append(group_queries(3))
+        grouped = grouped + [group_queries(b) for b in range(2, NB)]
         a.append(score(2, grouped[2]))
-        v_raw[2] = load_v(2, "q_grouped2")
-        e1 = exponentials(1, a[1])
+        e0 = exponentials(0, a[0])
         a.append(score(3, grouped[3]))
+        v_raw[0] = load_v(0, "q_grouped3")
+        e1 = exponentials(1, a[1])
+        v_raw[1] = load_v(1, "neg_max1")
         r0 = invert(0, e0[1])
         e2 = exponentials(2, a[2])
         weigh(0, e0[0], r0)
@@ -163,14 +169,15 @@ def tile_attend_unmerge_kernel(tc, query, keys_words, keys_scales, size, vals, o
         e3 = exponentials(3, a[3])
         r2 = invert(2, e2[1])
         weigh(1, e1[0], r1)
+        v_raw[2] = load_v(2, "p1")
         r3 = invert(3, e3[1])
         weigh(2, e2[0], r2)
         weigh(3, e3[0], r3)
-        rounded3 = cast_on_scalar(3, "neg_max3")
         g0 = turn_v(0, pick_on_vector(0, "p3"))
         w_quantised = quantise(w_grouped, "w")
         multiply(0, g0, w_quantised)
         g1 = turn_v(1, pick_on_vector(1, "v_grouped0"), "v0_codes")
+        rounded3 = cast_on_scalar(3, "p2")
         picked3 = sbuf([P, I], BF16, "v_picked3", after="v0_scales")
         pick_on_scalar(picked3, rounded3, 0)
         pick_on_scalar(picked3, rounded3, 256)
@@ -179,12 +186,12 @@ def tile_attend_unmerge_kernel(tc, query, keys_words, keys_scales, size, vals, o
         unmerge(0, 512, 512, "v0_codes")
         g3 = turn_v(3, picked3)
         g2 = turn_v(2, pick_on_vector(2, "o0"), "v1_codes")
+        multiply(3, g3, w_quantised, "p1")
         unmerge(1, 0, 512)
         multiply(2, g2, w_quantised)
-        multiply(3, g3, w_quantised, "q_grouped2")
         unmerge(1, 512, 512, "v1_codes")
-        unmerge(2, 0, 512)
-        unmerge(2, 512, 512)
         unmerge(3, 0, 512)
-        unmerge(3, 512, 256)
-        unmerge(3, 768, 256)
+        unmerge(3, 512, 512)
+        unmerge(2, 0, 512)
+        unmerge(2, 512, 256)
+        unmerge(2, 768, 256)

from contextlib import ExitStack

import concourse.mybir as mybir
from concourse.masks import make_identity

F32 = mybir.dt.float32
BF16 = mybir.dt.bfloat16
I32 = mybir.dt.int32
U32 = mybir.dt.uint32
U16 = mybir.dt.uint16
U8 = mybir.dt.uint8
FP8X4 = mybir.dt.float8_e4m3fn_x4
ACT = mybir.ActivationFunctionType
ALU = mybir.AluOpType
AXIS = mybir.AxisListType

P = 128
D, T, I, Q, E, M = 512, 2048, 512, 512, 512, 1024
FLOPS = 2 * D * Q * I + 2 * I * E * Q
NB = 4
SPARE = 16


def tile_attend_unmerge_kernel(tc, query, keys_words, keys_scales, size, vals, offs, offs2, out):
    nc = tc.nc
    with ExitStack() as ctx:
        held = ctx.enter_context(tc.tile_pool(name="held", bufs=1))
        psum = ctx.enter_context(tc.psum_pool(name="psum", bufs=1))
        acc_pool = ctx.enter_context(tc.psum_pool(name="acc", bufs=4))
        turn_pool = ctx.enter_context(tc.psum_pool(name="turn", bufs=3))

        def sbuf(shape, dtype, name, after=None):
            return held.tile(shape, dtype, name=name, tag=after or name, align_bytes=64)

        slots = held.tile([P, I // 16], U16, name="slots")
        rows = held.tile([P, M // 16], U16, name="rows")
        key_words = sbuf([P, T], U32, "key_words")
        key_bytes = sbuf([P, T], U8, "key_bytes")
        ident = sbuf([P, P], F32, "ident")
        scale_rows = sbuf([P, T], U8, "scale_rows")
        nc.gpsimd.memset(key_bytes[:].bitcast(I32), 0)
        make_identity(nc, ident[:])
        nc.sync.dma_start(slots[:], offs)
        for g, queue in enumerate([nc.scalar, nc.sync, nc.scalar, nc.sync]):
            queue.dma_start(scale_rows[32 * g : 32 * g + 4, :].bitcast(I32), keys_scales[0, 4 * g : 4 * g + 4, :].bitcast(I32))
        size_cols = sbuf([P, 4], F32, "size_cols")
        nc.scalar.dma_start(size_cols[:], size.rearrange("o (s t) -> (o s) t", t=4))
        nc.sync.dma_start(key_words[:].bitcast(I32), keys_words[0].rearrange("p n t -> p (n t)").bitcast(I32))
        q_view = query.rearrange("(p j) q -> p j q", j=4)
        q_raw = [sbuf([P, 4, Q // 2], F32, f"q_raw{h}") for h in range(2)]
        for h in range(2):
            nc.sync.dma_start(q_raw[h][:], q_view[:, :, h * (Q // 2) : (h + 1) * (Q // 2)])
        nc.sync.dma_start(rows[:], offs2)
        for g in range(4):
            nc.vector.tensor_copy(key_bytes[32 * g : 32 * g + 4, :].bitcast(I32), scale_rows[32 * g : 32 * g + 4, :].bitcast(I32))

        def load_v(j, after):
            raw = sbuf([P, T], F32, f"v_raw{j}", after=after)
            nc.sync.dma_start(raw[:], vals[j * P : (j + 1) * P, :])
            return raw

        o_tiles = [sbuf([P, Q + SPARE], F32, f"o{j}") for j in range(NB)]
        for j in range(NB):
            nc.gpsimd.memset(o_tiles[j][:, Q : Q + SPARE], 0.0)

        k_scales = sbuf([P, I], U8, "k_scales")
        nc.vector.tensor_copy(k_scales[:], key_bytes[:].indirect(slots[:]))
        k_codes = sbuf([P, I], U32, "k_codes", after="key_bytes")
        nc.vector.tensor_copy(k_codes[:], key_words[:].indirect(slots[:]))

        v_raw = {3: load_v(3, "key_words")}
        size_wide = psum.tile([P, I], F32, name="size_wide")
        for t in range(4):
            nc.tensor.transpose(size_wide[:, t:I:4], size_cols[:, t : t + 1].to_broadcast([P, P]), ident[:])

        def turn(src, dst):
            words = src[:].bitcast(F32)
            turned = turn_pool.tile([P, 2, P], F32, name="turned")
            for u in range(2):
                nc.tensor.transpose(turned[:, u, :], words[:, u : 2 * P : 2], ident[:])
            nc.scalar.copy(dst.bitcast(F32).rearrange("p (c u) -> p c u", u=2), turned[:].rearrange("p u c -> p c u"))

        def quantise(grouped, name, after=None):
            columns = grouped.shape[1] // 4
            codes = sbuf([P, columns], U32, name + "_codes", after=after)
            scales = sbuf([P, columns], U8, name + "_scales")
            nc.vector.quantize_mx(out=codes[:].bitcast(FP8X4), scales=scales[:], in_=grouped[:])
            return codes, scales

        def product(lhs, cols, rhs):
            acc = acc_pool.tile([P, 512], F32, name="acc")
            nc.tensor.matmul_mx(out=acc[:], lhsT=lhs[0][:, cols].bitcast(FP8X4), lhsT_scale=lhs[1][:, cols], rhs=rhs[0][:].bitcast(FP8X4), rhs_scale=rhs[1][:], start=True, stop=True)
            return acc

        def group_queries(b):
            grouped = sbuf([P, 4 * P], BF16, f"q_grouped{b}")
            src = q_raw[b // 2][:, :, (b % 2) * P : (b % 2 + 1) * P].rearrange("p j (c i) -> p c j i", i=4)
            dst = grouped[:].rearrange("p (c i j) -> p c j i", i=4, j=4)
            if b % 2 == 0:
                nc.vector.tensor_copy(dst, src)
            else:
                nc.scalar.activation(dst, src, ACT.Copy)
            return grouped

        def score(b, grouped):
            return product(quantise(grouped, f"q{b}"), slice(0, P), (k_codes, k_scales))

        def exponentials(b, a):
            neg_max = sbuf([P, 1], F32, f"neg_max{b}")
            nc.vector.tensor_reduce(neg_max[:], a[:], AXIS.X, ALU.max, negate=True)
            p = sbuf([P, I], F32, f"p{b}")
            total = sbuf([P, 1], F32, f"total{b}")
            nc.scalar.activation(p[:], a[:], ACT.Exp, bias=neg_max[:], accum_out=total[:])
            return p, total

        def invert(b, total):
            inverse = sbuf([P, 1], F32, f"inverse{b}")
            nc.vector.reciprocal(inverse[:], total[:])
            return inverse

        w_grouped = sbuf([P, 4 * Q], BF16, "w_grouped")

        def weigh(b, p, inverse):
            w = sbuf([P, I], BF16, f"w{b}")
            nc.vector.scalar_tensor_tensor(w[:], p[:], inverse[:], size_wide[:], ALU.mult, ALU.mult)
            turn(w, w_grouped[:, b * 4 * P : (b + 1) * 4 * P])

        def pick_on_vector(j, after):
            picked = sbuf([P, I], BF16, f"v_picked{j}", after=after)
            nc.vector.tensor_copy(picked[:], v_raw[j][:].indirect(slots[:]))
            return picked

        def cast_on_scalar(j, after):
            rounded = sbuf([P, T], BF16, f"v_rounded{j}", after=after)
            for c in range(0, T, 512):
                nc.scalar.activation(rounded[:, c : c + 512], v_raw[j][:, c : c + 512], ACT.Copy)
            return rounded

        def pick_on_scalar(picked, rounded, c):
            nc.scalar.activation(picked[:, c : c + 256], rounded[:].indirect(slots[:, c // 16 : (c + 256) // 16]), ACT.Copy)

        def turn_v(j, picked, after=None):
            grouped = sbuf([P, 4 * P], BF16, f"v_grouped{j}", after=after)
            turn(picked, grouped[:])
            return grouped

        def multiply(j, grouped, w_quantised, after=None):
            acc = product(quantise(grouped, f"v{j}", after), slice(0, P), w_quantised)
            nc.scalar.copy(o_tiles[j][:, 0:Q], acc[:])

        def unmerge(j, first, width, after=None):
            y = sbuf([P, width], F32, f"y{j}_{first}", after=after)
            nc.vector.tensor_copy(y[:], o_tiles[j][:].indirect(rows[:, first // 16 : (first + width) // 16]))
            nc.sync.dma_start(out[j * P : (j + 1) * P, first : first + width], y[:])

        grouped = [group_queries(b) for b in range(2)]
        a = [score(b, grouped[b]) for b in range(2)]
        grouped = grouped + [group_queries(b) for b in range(2, NB)]
        a.append(score(2, grouped[2]))
        e0 = exponentials(0, a[0])
        a.append(score(3, grouped[3]))
        v_raw[0] = load_v(0, "q_grouped3")
        e1 = exponentials(1, a[1])
        v_raw[1] = load_v(1, "neg_max1")
        r0 = invert(0, e0[1])
        e2 = exponentials(2, a[2])
        weigh(0, e0[0], r0)
        r1 = invert(1, e1[1])
        e3 = exponentials(3, a[3])
        r2 = invert(2, e2[1])
        weigh(1, e1[0], r1)
        v_raw[2] = load_v(2, "p1")
        r3 = invert(3, e3[1])
        weigh(2, e2[0], r2)
        weigh(3, e3[0], r3)
        g0 = turn_v(0, pick_on_vector(0, "p3"))
        w_quantised = quantise(w_grouped, "w")
        multiply(0, g0, w_quantised)
        g1 = turn_v(1, pick_on_vector(1, "v_grouped0"), "v0_codes")
        rounded3 = cast_on_scalar(3, "p2")
        picked3 = sbuf([P, I], BF16, "v_picked3", after="v0_scales")
        pick_on_scalar(picked3, rounded3, 0)
        pick_on_scalar(picked3, rounded3, 256)
        unmerge(0, 0, 512)
        multiply(1, g1, w_quantised)
        unmerge(0, 512, 512, "v0_codes")
        g3 = turn_v(3, picked3)
        g2 = turn_v(2, pick_on_vector(2, "o0"), "v1_codes")
        multiply(3, g3, w_quantised, "p1")
        unmerge(1, 0, 512)
        multiply(2, g2, w_quantised)
        unmerge(1, 512, 512, "v1_codes")
        unmerge(3, 0, 512)
        unmerge(3, 512, 512)
        unmerge(2, 0, 512)
        unmerge(2, 512, 256)
        unmerge(2, 768, 256)
